import numpy as np
import ml_dtypes


def mxq(x, axis, fmt="e4m3"):
    dtype, down = {"e4m3": (ml_dtypes.float8_e4m3fn, 7), "e5m2": (ml_dtypes.float8_e5m2, 14)}[fmt]
    v = np.moveaxis(np.asarray(x, np.float32).astype(ml_dtypes.bfloat16).astype(np.float64), axis, -1)
    blocks = v.reshape(v.shape[:-1] + (-1, 32))
    amax = np.abs(blocks).max(-1, keepdims=True)
    byte = np.maximum(np.where(amax > 0, np.frexp(amax)[1] - 1 + 127, 0) - down, 1)
    scale = np.exp2(byte - 127.0)
    codes = (blocks / scale).astype(np.float32).astype(dtype).astype(np.float64)
    return np.moveaxis((codes * scale).reshape(v.shape), -1, axis)


WIDE = False


def mx_kscale(k):
    if not WIDE:
        return np.ones(k)
    levels = np.array([10, -10, 5, -5, 0])
    if k % 512:
        return np.exp2(np.random.permutation(np.resize(levels, k // 32))).repeat(32)
    a = np.empty((k // 512, 16))
    for p in range(k // 512):
        a[p, :8] = np.random.permutation(np.resize(levels, 8))
        for g in range(8):
            far = levels[np.abs(levels - a[p, g]) >= 10]
            a[p, g + 8] = far[np.random.randint(len(far))]
    return np.exp2(a.ravel()).repeat(32)


def f64(x):
    return np.asarray(x).astype(np.float64)


def striped(idx):
    return np.tile(idx.reshape(-1, 16).T, (8, 1)).astype(np.uint16)


def unstriped(offs):
    return offs[:16].T.reshape(-1).astype(np.int64)


def striped8(idx):
    return np.concatenate([x.reshape(-1, 16).T for x in idx]).astype(np.uint16)


def runs(offs, k):
    lists = np.stack([offs[16 * r : 16 * r + 16].T.reshape(-1) for r in range(8)]).astype(np.int64)
    return lists[np.arange(k) % 512 // 64]


def pack_weight(w):
    k, n = w.shape
    w = f64(np.asarray(w, np.float32).astype(ml_dtypes.bfloat16)).reshape(k // 32, 32, n)
    amax = np.abs(w).max(1)
    byte = np.clip(np.where(amax > 0, np.frexp(amax)[1] - 1 + 127 - 7, 1), 1, 254)
    scaled = (w * np.exp2(127.0 - byte)[:, None, :]).reshape(k, n).astype(np.float32)
    words = np.ascontiguousarray(scaled.reshape(k // 512, 128, 4, n).transpose(0, 1, 3, 2)).astype(ml_dtypes.float8_e4m3fn).view(np.uint8)
    return words, np.ascontiguousarray(byte.astype(np.uint8).reshape(k // 512, 16, n))


def unpack_weight(words, scales):
    g, p, n, _ = words.shape
    vals = np.ascontiguousarray(words).view(ml_dtypes.float8_e4m3fn).astype(np.float64) * np.repeat(np.exp2(scales.astype(np.float64) - 127.0), 8, axis=1)[..., None]
    return vals.transpose(0, 1, 3, 2).reshape(g * 512, n)


def sigmoid(v):
    return 1.0 / (1.0 + np.exp(-np.maximum(v, -700.0)))

def planes(y):
    n, m = y.shape
    v = y.astype(np.float32).astype(ml_dtypes.bfloat16).astype(np.float64).reshape(n // 32, 32, m)
    top = np.abs(v).max(1)
    byte = np.clip(np.where(top > 0, np.frexp(top)[1] - 1 + 127 - 7, 1), 1, 254)
    codes = (v * np.exp2(127.0 - byte)[:, None, :]).reshape(n, m).astype(np.float32).astype(ml_dtypes.float8_e4m3fn).view(np.uint8)
    words = codes.reshape(n // 512, 128, 4, m).transpose(0, 1, 3, 2)
    return np.ascontiguousarray(words), np.ascontiguousarray(byte.astype(np.uint8).reshape(n // 512, 16, m))


K, T, S, G, H, J, C = 512, 1024, 256, 2048, 512, 512, 512


def setup_inputs():
    n = np.random.standard_normal
    s = mx_kscale(K)[:, None]
    packed_xT = pack_weight(n((K, T)) * s)
    packed_dT = pack_weight(n((K, G)) / s)
    return {
        "x_words": packed_xT[0],
        "x_scales": packed_xT[1],
        "d_words": packed_dT[0],
        "d_scales": packed_dT[1],
        "tab": n((H, J)).astype(np.float32),
        "sl": np.random.uniform(1.0, 2.0, (H, 1)).astype(np.float32),
        "th": (0.5 * n((H, 1))).astype(np.float32),
        "gs": (np.random.uniform(0.5, 1.5, (K, 1)) / s).astype(np.float32),
        "sl2": np.random.uniform(1.0, 2.0, (H, 1)).astype(np.float32),
        "th2": (0.5 * n((H, 1))).astype(np.float32),
        "offs": striped(np.random.permutation(T)[:S]),
        "k1": striped8(np.random.randint(0, G, (8, H))),
        "n1": striped8(np.random.randint(0, J, (8, S))),
        "n2": striped8(np.stack([np.random.permutation(S) for _ in range(8)])),
        "cand": striped(np.random.permutation(T)[:C]),
        "two": striped(np.random.permutation(T)[:S]),
        "k2": striped8(np.random.randint(0, G, (8, H))),
        "n3": striped(np.random.permutation(S)),
        "n4": striped(np.random.permutation(S)),
    }


def reference(x_words, x_scales, d_words, d_scales, tab, sl, th, gs, sl2, th2, offs, k1, n1, n2, cand, two, k2, n3, n4):
    x_cand = unpack_weight(x_words, x_scales)[:, unstriped(cand)]
    d_k1 = unpack_weight(d_words, d_scales)[np.arange(K)[:, None], runs(k1, K)]
    xq = unpack_weight(x_words, x_scales)[:, unstriped(offs)]
    h = 0.0625 * (d_k1.T @ xq)
    sg = sigmoid(f64(sl) * (f64(tab)[np.arange(H)[:, None], runs(n1, H)] - f64(th)))
    z = f64(gs) * (h * sg - (0.5 * (h[np.arange(H)[:, None], runs(n2, H)])))
    a = 0.0625 * ((x_cand.T @ mxq(z, 0, "e4m3")))
    d_k2 = unpack_weight(d_words, d_scales)[np.arange(K)[:, None], runs(k2, K)]
    x_two = unpack_weight(x_words, x_scales)[:, unstriped(two)]
    b = 0.0625 * (d_k2.T @ x_two)
    sg2 = sigmoid(f64(sl2) * (b[:, unstriped(n3)] - f64(th2)))
    out_0 = np.maximum(a * sg2, b[:, unstriped(n4)] - b)
    return (out_0,) + planes(out_0)

@@ -1,0 +1,231 @@
+from contextlib import ExitStack
+
+import concourse.mybir as mybir
+
+K, T, S, G, H, J, C = 512, 1024, 256, 2048, 512, 512, 512
+FLOPS = 2 * K * S * (H + C + H)
+
+F32 = mybir.dt.float32
+BF16 = mybir.dt.bfloat16
+I32 = mybir.dt.int32
+U32 = mybir.dt.uint32
+U16 = mybir.dt.uint16
+U8 = mybir.dt.uint8
+FP8X4 = mybir.dt.float8_e4m3fn_x4
+MULT = mybir.AluOpType.mult
+ADD = mybir.AluOpType.add
+MAX = mybir.AluOpType.max
+COPY = mybir.ActivationFunctionType.Copy
+SIGMOID = mybir.ActivationFunctionType.Sigmoid
+
+P = 128
+PACK = 4
+HALVES = 2
+W = S // HALVES
+LIST_ROWS = 16
+
+
+def tile_picked_pqcjmxbekd_none_po_kernel(
+    tc, x_words, x_scales, d_words, d_scales, tab, sl, th, gs, sl2, th2,
+    offs, k1, n1, n2, cand, two, k2, n3, n4, out_0, out_1, out_2,
+):
+    nc = tc.nc
+    with ExitStack() as ctx:
+        keep = ctx.enter_context(tc.tile_pool(name="keep", bufs=1))
+        psum = ctx.enter_context(tc.psum_pool(name="psum", bufs=1))
+
+        def sb(name, shape, dtype):
+            return keep.tile(shape, dtype, name=name, align_bytes=64)
+
+        def load_list(name, src):
+            t = keep.tile(list(src.shape), U16, name=name)
+            nc.sync.dma_start(t[:], src)
+            return t
+
+        def load_rows(name, src):
+            t = sb(name, [P, PACK], F32)
+            nc.gpsimd.dma_start(out=t[:], in_=src.rearrange("(p t) o -> p (t o)", t=PACK))
+            return t
+
+        def dealt(ap):
+            return ap.rearrange("p (t m) -> p m t", t=PACK)
+
+        def listed(ap):
+            return ap.rearrange("p (m t) -> p m t", t=PACK)
+
+        d_byte_win = sb("d_byte_win", [P, G], U8)
+        x_byte_win = sb("x_byte_win", [P, T], U8)
+        nc.vector.memset(d_byte_win[:].bitcast(I32), 0)
+        nc.vector.memset(x_byte_win[:].bitcast(I32), 0)
+
+        d_word_win = sb("d_word_win", [P, G], U32)
+        x_word_win = sb("x_word_win", [P, T], U32)
+        k1_t = load_list("k1_t", k1)
+        k2_t = load_list("k2_t", k2)
+        offs_t = load_list("offs_t", offs)
+        nc.sync.dma_start(out=x_word_win[:].bitcast(I32), in_=x_words[0].rearrange("p n t -> p (n t)").bitcast(I32))
+        nc.scalar.dma_start(out=d_byte_win[:].bitcast(I32)[0:P:8, :], in_=d_scales[0].bitcast(I32))
+        x_rows = x_scales[0].bitcast(I32)
+        for q in range(4):
+            nc.scalar.dma_start(out=x_byte_win[:].bitcast(I32)[32 * q : 32 * q + 4, :], in_=x_rows[4 * q : 4 * q + 4, :])
+        nc.sync.dma_start(out=d_word_win[:].bitcast(I32), in_=d_words[0].rearrange("p n t -> p (n t)").bitcast(I32))
+        n1_t = load_list("n1_t", n1)
+        tab_rows = tab.rearrange("(p t) j -> p t j", t=PACK)
+        tab_win = [sb("tab_win%d" % t, [P, J], F32) for t in range(PACK)]
+        nc.sync.dma_start(out=tab_win[0][:], in_=tab_rows[:, 0, :])
+        two_t = load_list("two_t", two)
+        for t in range(1, PACK):
+            nc.sync.dma_start(out=tab_win[t][:], in_=tab_rows[:, t, :])
+        cand_t = load_list("cand_t", cand)
+        n2_t = load_list("n2_t", n2)
+        n3_t = load_list("n3_t", n3)
+        n4_t = load_list("n4_t", n4)
+
+        sl_t = load_rows("sl_t", sl)
+        th_t = load_rows("th_t", th)
+        gs_t = load_rows("gs_t", gs)
+        sl2_t = load_rows("sl2_t", sl2)
+        th2_t = load_rows("th2_t", th2)
+
+        def minus_product(name, u, v):
+            prod = sb(name + "_pos", [P, PACK], F32)
+            nc.gpsimd.tensor_tensor(prod[:], u[:], v[:], MULT)
+            neg = sb(name, [P, PACK], F32)
+            nc.gpsimd.tensor_scalar(neg[:], prod[:], -1.0, 0.0, MULT, ADD)
+            return neg
+
+        bias1 = minus_product("bias1", sl_t, th_t)
+        w_gain = sb("w_gain", [P, PACK], F32)
+        nc.gpsimd.tensor_scalar(w_gain[:], gs_t[:], -0.5 * 0.0625, 0.0, MULT, ADD)
+        bias2 = minus_product("bias2", sl2_t, th2_t)
+
+        d_bytes = sb("d_bytes", [P, 2, H], U8)
+        nc.vector.tensor_copy(d_bytes[:, 0, :], d_byte_win[:].indirect(k1_t[:]))
+        nc.vector.tensor_copy(d_bytes[:, 1, :], d_byte_win[:].indirect(k2_t[:]))
+        d_plane = sb("d_plane", [P, 2, H], U8)
+        nc.vector.tensor_copy(
+            d_plane[:].rearrange("p l (t m) -> p l m t", t=PACK),
+            d_bytes[:].rearrange("p l (m t) -> p l m t", t=PACK),
+        )
+        d_plane_i = d_plane[:].rearrange("p l h -> p (l h)").bitcast(I32)
+        for r in range(1, 4):
+            nc.sync.dma_start(out=d_plane_i[r:P:32, :], in_=d_plane_i[8 * r : P : 32, :])
+
+        def coded_matrix(name, list_t):
+            picked = sb(name + "_picked", [P, H], U32)
+            nc.vector.tensor_copy(picked[:], d_word_win[:].indirect(list_t[:]))
+            words = sb(name + "_words", [P, H], U32)
+            nc.vector.tensor_copy(dealt(words[:]), listed(picked[:]))
+            return words
+
+        def tokens(name, list_t):
+            plane = sb(name + "_plane", [P, S], U8)
+            nc.vector.tensor_copy(plane[:], x_byte_win[:].indirect(list_t[:]))
+            words = sb(name + "_words", [P, S], U32)
+            nc.vector.tensor_copy(words[:], x_word_win[:].indirect(list_t[:]))
+            return words, plane
+
+        def product(out, words, plane, t, rhs_words, rhs_plane):
+            cols = slice(t * P, (t + 1) * P)
+            nc.tensor.matmul_mx(
+                out=out, lhsT=words[:, cols].bitcast(FP8X4), lhsT_scale=plane[:, cols],
+                rhs=rhs_words.bitcast(FP8X4), rhs_scale=rhs_plane, start=True, stop=True,
+            )
+
+        xq_words, xq_plane = tokens("xq", offs_t)
+        k1_words = coded_matrix("k1", k1_t)
+        h_ps = [psum.tile([P, S], F32, name="h_ps%d" % t) for t in range(PACK)]
+        for t in range(PACK):
+            product(h_ps[t][:], k1_words, d_plane[:, 0, :], t, xq_words[:], xq_plane[:])
+
+        k2_words = coded_matrix("k2", k2_t)
+        x2_words, x2_plane = tokens("x2", two_t)
+        b_ps = [psum.tile([P, 2, S], F32, name="b_ps%d" % u) for u in range(2)]
+        for t in range(PACK):
+            product(b_ps[t // 2][:, t % 2, :], k2_words, d_plane[:, 1, :], t, x2_words[:], x2_plane[:])
+
+        cand_plane = sb("cand_plane", [P, C], U8)
+        nc.vector.tensor_copy(dealt(cand_plane[:]), x_byte_win[:].indirect(cand_t[:]))
+        cand_words = sb("cand_words", [P, C], U32)
+        nc.vector.tensor_copy(dealt(cand_words[:]), x_word_win[:].indirect(cand_t[:]))
+
+        sg = sb("sg", [P, PACK, S], F32)
+        for t in range(PACK):
+            nc.scalar.activation(
+                sg[:, t, :], tab_win[t][:].indirect(n1_t[:]), SIGMOID,
+                bias=bias1[:, t : t + 1], scale=sl_t[:, t : t + 1],
+            )
+
+        w_win = [sb("w_win%d" % t, [P, S], F32) for t in range(PACK)]
+        gated = sb("gated", [P, HALVES, PACK, W], F32)
+        for t in range(PACK):
+            nc.scalar.activation(w_win[t][:], h_ps[t][:], COPY, scale=w_gain[:, t : t + 1])
+            nc.vector.scalar_tensor_tensor(
+                gated[:, :, t, :], w_win[t][:].rearrange("p (u j) -> p u j", u=HALVES), -2.0,
+                sg[:, t, :].rearrange("p (u j) -> p u j", u=HALVES), MULT, MULT,
+            )
+
+        def half(list_t, u):
+            n = W // LIST_ROWS
+            return list_t[:, u * n : (u + 1) * n]
+
+        def woven_out(ap):
+            return ap.rearrange("p (c i t) -> p c t i", i=4, t=PACK)
+
+        def woven_in(ap):
+            return ap.rearrange("p t (c i) -> p c t i", i=4)
+
+        a_ps = []
+        for u in range(HALVES):
+            w_n2 = sb("w_n2_%d" % u, [P, PACK, W], F32)
+            for t in range(PACK):
+                nc.scalar.activation(w_n2[:, t, :], w_win[t][:].indirect(half(n2_t, u)), COPY)
+            z_bf = sb("z_bf%d" % u, [P, PACK * W], BF16)
+            nc.vector.tensor_tensor(woven_out(z_bf[:]), woven_in(gated[:, u, :, :]), woven_in(w_n2[:]), ADD)
+            z_words = sb("z_words%d" % u, [P, W], U32)
+            z_plane = sb("z_plane%d" % u, [P, W], U8)
+            nc.vector.quantize_mx(out=z_words[:].bitcast(FP8X4), scales=z_plane[:], in_=z_bf[:])
+            acc = psum.tile([P, PACK, W], F32, name="a_ps%d" % u)
+            for t in range(PACK):
+                product(acc[:, t, :], cand_words, cand_plane, t, z_words[:], z_plane[:])
+            a_ps.append(acc)
+
+        b_win = [sb("b_win%d" % t, [P, S], F32) for t in range(PACK)]
+        for t in range(PACK):
+            nc.scalar.activation(b_win[t][:], b_ps[t // 2][:, t % 2, :], COPY, scale=0.0625)
+
+        y_words = sb("y_words", [P, S], U32)
+        y_plane = sb("y_plane", [P, S], U8)
+        out_rows = out_0.rearrange("(p t) j -> p t j", t=PACK)
+        out_words = out_1[0].rearrange("p n t -> p (n t)").bitcast(I32)
+        for u in range(HALVES):
+            cols = slice(u * W, (u + 1) * W)
+            sg2 = sb("sg2_%d" % u, [P, PACK, W], F32)
+            for t in range(PACK):
+                nc.scalar.activation(
+                    sg2[:, t, :], b_win[t][:].indirect(half(n3_t, u)), SIGMOID,
+                    bias=bias2[:, t : t + 1], scale=sl2_t[:, t : t + 1],
+                )
+            b_n4 = sb("b_n4_%d" % u, [P, PACK, W], F32)
+            for t in range(PACK):
+                nc.scalar.activation(b_n4[:, t, :], b_win[t][:].indirect(half(n4_t, u)), COPY)
+            score = sb("score%d" % u, [P, PACK, W], F32)
+            nc.vector.scalar_tensor_tensor(score[:], a_ps[u][:], 0.0625, sg2[:], MULT, MULT)
+            diff = sb("diff%d" % u, [P, PACK, W], F32)
+            for v in range(2):
+                nc.vector.scalar_tensor_tensor(
+                    diff[:, 2 * v : 2 * v + 2, :], b_ps[v][:, :, cols], -0.0625, b_n4[:, 2 * v : 2 * v + 2, :], MULT, ADD,
+                )
+            y = sb("y%d" % u, [P, PACK, W], F32)
+            nc.vector.tensor_tensor(y[:], score[:], diff[:], MAX)
+            nc.sync.dma_start(out=out_rows[:, :, cols], in_=y[:])
+            y_bf = sb("y_bf%d" % u, [P, PACK * W], BF16)
+            nc.vector.tensor_copy(woven_out(y_bf[:]), woven_in(y[:]))
+            nc.vector.quantize_mx(out=y_words[:, cols].bitcast(FP8X4), scales=y_plane[:, cols], in_=y_bf[:])
+            nc.sync.dma_start(out=out_words[:, cols], in_=y_words[:, cols].bitcast(I32))
+
+        out_scale_rows = out_2[0].bitcast(I32)
+        y_plane_i = y_plane[:].bitcast(I32)
+        for q in range(4):
+            eng = nc.scalar if q % 2 else nc.sync
+            eng.dma_start(out=out_scale_rows[4 * q : 4 * q + 4, :], in_=y_plane_i[32 * q : 32 * q + 4, :])

@@ -32,19 +32,23 @@ def tile_picked_pqcjmxbekd_none_po_kernel(
     nc = tc.nc
     with ExitStack() as ctx:
         keep = ctx.enter_context(tc.tile_pool(name="keep", bufs=1))
+        reuse = ctx.enter_context(tc.tile_pool(name="reuse", bufs=1))
         psum = ctx.enter_context(tc.psum_pool(name="psum", bufs=1))
 
-        def sb(name, shape, dtype):
-            return keep.tile(shape, dtype, name=name, align_bytes=64)
+        def sb(name, shape, dtype, tag=None):
+            return keep.tile(shape, dtype, name=name, tag=tag or name, align_bytes=64)
+
+        def at(offset, name, shape, dtype):
+            return reuse.tile(shape, dtype, name=name, offset=offset, align_bytes=64)
 
         def load_list(name, src):
             t = keep.tile(list(src.shape), U16, name=name)
             nc.sync.dma_start(t[:], src)
             return t
 
-        def load_rows(name, src):
+        def load_rows(eng, name, src):
             t = sb(name, [P, PACK], F32)
-            nc.gpsimd.dma_start(out=t[:], in_=src.rearrange("(p t) o -> p (t o)", t=PACK))
+            eng.dma_start(out=t[:], in_=src.rearrange("(p t) o -> p (t o)", t=PACK))
             return t
 
         def dealt(ap):
@@ -55,37 +59,40 @@ def tile_picked_pqcjmxbekd_none_po_kernel(
 
         d_byte_win = sb("d_byte_win", [P, G], U8)
         x_byte_win = sb("x_byte_win", [P, T], U8)
-        nc.vector.memset(d_byte_win[:].bitcast(I32), 0)
         nc.vector.memset(x_byte_win[:].bitcast(I32), 0)
 
+        row_win = [sb("row_win%d" % t, [P, 2 * S], F32) for t in range(PACK)]
         d_word_win = sb("d_word_win", [P, G], U32)
         x_word_win = sb("x_word_win", [P, T], U32)
         k1_t = load_list("k1_t", k1)
+        nc.sync.dma_start(
+            out=d_byte_win[:].bitcast(I32),
+            in_=d_scales[0].bitcast(I32).unsqueeze(1).to_broadcast([16, 8, G // 4]),
+        )
         k2_t = load_list("k2_t", k2)
-        offs_t = load_list("offs_t", offs)
-        nc.sync.dma_start(out=x_word_win[:].bitcast(I32), in_=x_words[0].rearrange("p n t -> p (n t)").bitcast(I32))
-        nc.scalar.dma_start(out=d_byte_win[:].bitcast(I32)[0:P:8, :], in_=d_scales[0].bitcast(I32))
-        x_rows = x_scales[0].bitcast(I32)
-        for q in range(4):
-            nc.scalar.dma_start(out=x_byte_win[:].bitcast(I32)[32 * q : 32 * q + 4, :], in_=x_rows[4 * q : 4 * q + 4, :])
-        nc.sync.dma_start(out=d_word_win[:].bitcast(I32), in_=d_words[0].rearrange("p n t -> p (n t)").bitcast(I32))
+        sl_t = load_rows(nc.sync, "sl_t", sl)
+        th_t = load_rows(nc.sync, "th_t", th)
         n1_t = load_list("n1_t", n1)
         tab_rows = tab.rearrange("(p t) j -> p t j", t=PACK)
-        tab_win = [sb("tab_win%d" % t, [P, J], F32) for t in range(PACK)]
+        tab_win = [sb("tab_win%d" % t, [P, J], F32) for t in range(PACK - 1)]
         nc.sync.dma_start(out=tab_win[0][:], in_=tab_rows[:, 0, :])
-        two_t = load_list("two_t", two)
-        for t in range(1, PACK):
-            nc.sync.dma_start(out=tab_win[t][:], in_=tab_rows[:, t, :])
-        cand_t = load_list("cand_t", cand)
+        nc.sync.dma_start(out=x_word_win[:].bitcast(I32), in_=x_words[0].rearrange("p n t -> p (n t)").bitcast(I32))
+        offs_t = load_list("offs_t", offs)
+        x_rows = x_scales[0].bitcast(I32)
+        for q in range(4):
+            nc.sync.dma_start(out=x_byte_win[:].bitcast(I32)[32 * q : 32 * q + 4, :], in_=x_rows[4 * q : 4 * q + 4, :])
+        nc.sync.dma_start(out=d_word_win[:].bitcast(I32), in_=d_words[0].rearrange("p n t -> p (n t)").bitcast(I32))
         n2_t = load_list("n2_t", n2)
         n3_t = load_list("n3_t", n3)
         n4_t = load_list("n4_t", n4)
+        two_t = load_list("two_t", two)
+        cand_t = load_list("cand_t", cand)
+        for t in range(1, PACK - 1):
+            nc.sync.dma_start(out=tab_win[t][:], in_=tab_rows[:, t, :])
 
-        sl_t = load_rows("sl_t", sl)
-        th_t = load_rows("th_t", th)
-        gs_t = load_rows("gs_t", gs)
-        sl2_t = load_rows("sl2_t", sl2)
-        th2_t = load_rows("th2_t", th2)
+        gs_t = load_rows(nc.gpsimd, "gs_t", gs)
+        sl2_t = load_rows(nc.gpsimd, "sl2_t", sl2)
+        th2_t = load_rows(nc.gpsimd, "th2_t", th2)
 
         def minus_product(name, u, v):
             prod = sb(name + "_pos", [P, PACK], F32)
@@ -94,12 +101,18 @@ def tile_picked_pqcjmxbekd_none_po_kernel(
             nc.gpsimd.tensor_scalar(neg[:], prod[:], -1.0, 0.0, MULT, ADD)
             return neg
 
-        bias1 = minus_product("bias1", sl_t, th_t)
+        bias1 = sb("bias1", [P, PACK], F32)
+        nc.vector.scalar_tensor_tensor(bias1[:], sl_t[:], -1.0, th_t[:], MULT, MULT)
         w_gain = sb("w_gain", [P, PACK], F32)
         nc.gpsimd.tensor_scalar(w_gain[:], gs_t[:], -0.5 * 0.0625, 0.0, MULT, ADD)
+        h_gain = sb("h_gain", [P, PACK], F32)
+        nc.gpsimd.tensor_scalar(h_gain[:], gs_t[:], 0.0625, 0.0, MULT, ADD)
         bias2 = minus_product("bias2", sl2_t, th2_t)
 
-        d_bytes = sb("d_bytes", [P, 2, H], U8)
+        for t in range(PACK):
+            nc.vector.memset(row_win[t][:, S:], 0.0)
+
+        d_bytes = at(4096, "d_bytes", [P, 2, H], U8)
         nc.vector.tensor_copy(d_bytes[:, 0, :], d_byte_win[:].indirect(k1_t[:]))
         nc.vector.tensor_copy(d_bytes[:, 1, :], d_byte_win[:].indirect(k2_t[:]))
         d_plane = sb("d_plane", [P, 2, H], U8)
@@ -111,19 +124,18 @@ def tile_picked_pqcjmxbekd_none_po_kernel(
         for r in range(1, 4):
             nc.sync.dma_start(out=d_plane_i[r:P:32, :], in_=d_plane_i[8 * r : P : 32, :])
 
-        def coded_matrix(name, list_t):
-            picked = sb(name + "_picked", [P, H], U32)
+        tab_win.append(at(4096, "tab_win3", [P, J], F32))
+        nc.sync.dma_start(out=tab_win[3][:], in_=tab_rows[:, 3, :])
+
+        def coded_matrix(name, list_t, picked):
             nc.vector.tensor_copy(picked[:], d_word_win[:].indirect(list_t[:]))
             words = sb(name + "_words", [P, H], U32)
             nc.vector.tensor_copy(dealt(words[:]), listed(picked[:]))
             return words
 
-        def tokens(name, list_t):
-            plane = sb(name + "_plane", [P, S], U8)
+        def tokens(list_t, words, plane):
             nc.vector.tensor_copy(plane[:], x_byte_win[:].indirect(list_t[:]))
-            words = sb(name + "_words", [P, S], U32)
             nc.vector.tensor_copy(words[:], x_word_win[:].indirect(list_t[:]))
-            return words, plane
 
         def product(out, words, plane, t, rhs_words, rhs_plane):
             cols = slice(t * P, (t + 1) * P)
@@ -132,21 +144,25 @@ def tile_picked_pqcjmxbekd_none_po_kernel(
                 rhs=rhs_words.bitcast(FP8X4), rhs_scale=rhs_plane, start=True, stop=True,
             )
 
-        xq_words, xq_plane = tokens("xq", offs_t)
-        k1_words = coded_matrix("k1", k1_t)
+        xq_words = sb("xq_words", [P, S], U32)
+        xq_plane = sb("xq_plane", [P, S], U8)
+        tokens(offs_t, xq_words, xq_plane)
+        k1_words = coded_matrix("k1", k1_t, at(0, "k1_picked", [P, H], U32))
         h_ps = [psum.tile([P, S], F32, name="h_ps%d" % t) for t in range(PACK)]
         for t in range(PACK):
             product(h_ps[t][:], k1_words, d_plane[:, 0, :], t, xq_words[:], xq_plane[:])
 
-        k2_words = coded_matrix("k2", k2_t)
-        x2_words, x2_plane = tokens("x2", two_t)
+        k2_words = coded_matrix("k2", k2_t, at(4 * S + S + C, "k2_picked", [P, H], U32))
+        x2_words = at(0, "x2_words", [P, S], U32)
+        x2_plane = at(4 * S, "x2_plane", [P, S], U8)
+        tokens(two_t, x2_words, x2_plane)
         b_ps = [psum.tile([P, 2, S], F32, name="b_ps%d" % u) for u in range(2)]
         for t in range(PACK):
             product(b_ps[t // 2][:, t % 2, :], k2_words, d_plane[:, 1, :], t, x2_words[:], x2_plane[:])
 
-        cand_plane = sb("cand_plane", [P, C], U8)
+        cand_plane = at(4 * S + S, "cand_plane", [P, C], U8)
         nc.vector.tensor_copy(dealt(cand_plane[:]), x_byte_win[:].indirect(cand_t[:]))
-        cand_words = sb("cand_words", [P, C], U32)
+        cand_words = at(4 * S + S + C, "cand_words", [P, C], U32)
         nc.vector.tensor_copy(dealt(cand_words[:]), x_word_win[:].indirect(cand_t[:]))
 
         sg = sb("sg", [P, PACK, S], F32)
@@ -156,18 +172,13 @@ def tile_picked_pqcjmxbekd_none_po_kernel(
                 bias=bias1[:, t : t + 1], scale=sl_t[:, t : t + 1],
             )
 
-        w_win = [sb("w_win%d" % t, [P, S], F32) for t in range(PACK)]
-        gated = sb("gated", [P, HALVES, PACK, W], F32)
+        gated = sb("gated", [P, PACK, S], F32)
+        w_n2 = sb("w_n2", [P, PACK, S], F32)
         for t in range(PACK):
-            nc.scalar.activation(w_win[t][:], h_ps[t][:], COPY, scale=w_gain[:, t : t + 1])
-            nc.vector.scalar_tensor_tensor(
-                gated[:, :, t, :], w_win[t][:].rearrange("p (u j) -> p u j", u=HALVES), -2.0,
-                sg[:, t, :].rearrange("p (u j) -> p u j", u=HALVES), MULT, MULT,
-            )
-
-        def half(list_t, u):
-            n = W // LIST_ROWS
-            return list_t[:, u * n : (u + 1) * n]
+            nc.scalar.activation(row_win[t][:, :S], h_ps[t][:], COPY, scale=w_gain[:, t : t + 1])
+            nc.vector.scalar_tensor_tensor(gated[:, t, :], h_ps[t][:], h_gain[:, t : t + 1], sg[:, t, :], MULT, MULT)
+        for t in range(PACK):
+            nc.scalar.activation(w_n2[:, t, :], row_win[t][:].indirect(n2_t[:]), COPY)
 
         def woven_out(ap):
             return ap.rearrange("p (c i t) -> p c t i", i=4, t=PACK)
@@ -175,24 +186,24 @@ def tile_picked_pqcjmxbekd_none_po_kernel(
         def woven_in(ap):
             return ap.rearrange("p t (c i) -> p c t i", i=4)
 
-        a_ps = []
-        for u in range(HALVES):
-            w_n2 = sb("w_n2_%d" % u, [P, PACK, W], F32)
-            for t in range(PACK):
-                nc.scalar.activation(w_n2[:, t, :], w_win[t][:].indirect(half(n2_t, u)), COPY)
-            z_bf = sb("z_bf%d" % u, [P, PACK * W], BF16)
-            nc.vector.tensor_tensor(woven_out(z_bf[:]), woven_in(gated[:, u, :, :]), woven_in(w_n2[:]), ADD)
-            z_words = sb("z_words%d" % u, [P, W], U32)
-            z_plane = sb("z_plane%d" % u, [P, W], U8)
-            nc.vector.quantize_mx(out=z_words[:].bitcast(FP8X4), scales=z_plane[:], in_=z_bf[:])
-            acc = psum.tile([P, PACK, W], F32, name="a_ps%d" % u)
-            for t in range(PACK):
-                product(acc[:, t, :], cand_words, cand_plane, t, z_words[:], z_plane[:])
-            a_ps.append(acc)
-
-        b_win = [sb("b_win%d" % t, [P, S], F32) for t in range(PACK)]
+        z_bf = sb("z_bf", [P, PACK * S], BF16)
+        nc.vector.tensor_tensor(woven_out(z_bf[:]), woven_in(gated[:]), woven_in(w_n2[:]), ADD)
+        z_words = sb("z_words", [P, S], U32)
+        z_plane = sb("z_plane", [P, S], U8)
+        nc.vector.quantize_mx(out=z_words[:].bitcast(FP8X4), scales=z_plane[:], in_=z_bf[:])
+        a_ps = [psum.tile([P, 2, S], F32, name="a_ps%d" % v) for v in range(2)]
         for t in range(PACK):
-            nc.scalar.activation(b_win[t][:], b_ps[t // 2][:, t % 2, :], COPY, scale=0.0625)
+            product(a_ps[t // 2][:, t % 2, :], cand_words, cand_plane, t, z_words[:], z_plane[:])
+
+        for t in range(PACK):
+            nc.scalar.activation(row_win[t][:, :S], b_ps[t // 2][:, t % 2, :], COPY, scale=0.0625)
+        b_n4 = sb("b_n4", [P, PACK, S], F32)
+        diff = sb("diff", [P, PACK, S], F32)
+        for v in range(2):
+            pair = slice(2 * v, 2 * v + 2)
+            for t in range(2 * v, 2 * v + 2):
+                nc.scalar.activation(b_n4[:, t, :], row_win[t][:].indirect(n4_t[:]), COPY)
+            nc.vector.scalar_tensor_tensor(diff[:, pair, :], b_ps[v][:], -0.0625, b_n4[:, pair, :], MULT, ADD)
 
         y_words = sb("y_words", [P, S], U32)
         y_plane = sb("y_plane", [P, S], U8)
@@ -200,24 +211,19 @@ def tile_picked_pqcjmxbekd_none_po_kernel(
         out_words = out_1[0].rearrange("p n t -> p (n t)").bitcast(I32)
         for u in range(HALVES):
             cols = slice(u * W, (u + 1) * W)
+            n3_half = n3_t[:, u * (W // LIST_ROWS) : (u + 1) * (W // LIST_ROWS)]
             sg2 = sb("sg2_%d" % u, [P, PACK, W], F32)
-            for t in range(PACK):
-                nc.scalar.activation(
-                    sg2[:, t, :], b_win[t][:].indirect(half(n3_t, u)), SIGMOID,
-                    bias=bias2[:, t : t + 1], scale=sl2_t[:, t : t + 1],
-                )
-            b_n4 = sb("b_n4_%d" % u, [P, PACK, W], F32)
-            for t in range(PACK):
-                nc.scalar.activation(b_n4[:, t, :], b_win[t][:].indirect(half(n4_t, u)), COPY)
             score = sb("score%d" % u, [P, PACK, W], F32)
-            nc.vector.scalar_tensor_tensor(score[:], a_ps[u][:], 0.0625, sg2[:], MULT, MULT)
-            diff = sb("diff%d" % u, [P, PACK, W], F32)
-            for v in range(2):
-                nc.vector.scalar_tensor_tensor(
-                    diff[:, 2 * v : 2 * v + 2, :], b_ps[v][:, :, cols], -0.0625, b_n4[:, 2 * v : 2 * v + 2, :], MULT, ADD,
-                )
             y = sb("y%d" % u, [P, PACK, W], F32)
-            nc.vector.tensor_tensor(y[:], score[:], diff[:], MAX)
+            for v in range(2):
+                pair = slice(2 * v, 2 * v + 2)
+                for t in range(2 * v, 2 * v + 2):
+                    nc.scalar.activation(
+                        sg2[:, t, :], row_win[t][:].indirect(n3_half), SIGMOID,
+                        bias=bias2[:, t : t + 1], scale=sl2_t[:, t : t + 1],
+                    )
+                nc.vector.scalar_tensor_tensor(score[:, pair, :], a_ps[v][:, :, cols], 0.0625, sg2[:, pair, :], MULT, MULT)
+                nc.vector.tensor_tensor(y[:, pair, :], score[:, pair, :], diff[:, pair, cols], MAX)
             nc.sync.dma_start(out=out_rows[:, :, cols], in_=y[:])
             y_bf = sb("y_bf%d" % u, [P, PACK * W], BF16)
             nc.vector.tensor_copy(woven_out(y_bf[:]), woven_in(y[:]))

@@ -14,6 +14,7 @@ U8 = mybir.dt.uint8
 FP8X4 = mybir.dt.float8_e4m3fn_x4
 MULT = mybir.AluOpType.mult
 ADD = mybir.AluOpType.add
+SUBTRACT = mybir.AluOpType.subtract
 MAX = mybir.AluOpType.max
 COPY = mybir.ActivationFunctionType.Copy
 SIGMOID = mybir.ActivationFunctionType.Sigmoid
@@ -103,8 +104,6 @@ def tile_picked_pqcjmxbekd_none_po_kernel(
 
         bias1 = sb("bias1", [P, PACK], F32)
         nc.vector.scalar_tensor_tensor(bias1[:], sl_t[:], -1.0, th_t[:], MULT, MULT)
-        w_gain = sb("w_gain", [P, PACK], F32)
-        nc.gpsimd.tensor_scalar(w_gain[:], gs_t[:], -0.5 * 0.0625, 0.0, MULT, ADD)
         h_gain = sb("h_gain", [P, PACK], F32)
         nc.gpsimd.tensor_scalar(h_gain[:], gs_t[:], 0.0625, 0.0, MULT, ADD)
         bias2 = minus_product("bias2", sl2_t, th2_t)
@@ -175,10 +174,10 @@ def tile_picked_pqcjmxbekd_none_po_kernel(
         gated = sb("gated", [P, PACK, S], F32)
         w_n2 = sb("w_n2", [P, PACK, S], F32)
         for t in range(PACK):
-            nc.scalar.activation(row_win[t][:, :S], h_ps[t][:], COPY, scale=w_gain[:, t : t + 1])
-            nc.vector.scalar_tensor_tensor(gated[:, t, :], h_ps[t][:], h_gain[:, t : t + 1], sg[:, t, :], MULT, MULT)
+            nc.scalar.activation(row_win[t][:, :S], h_ps[t][:], COPY, scale=h_gain[:, t : t + 1])
+            nc.gpsimd.tensor_tensor(gated[:, t, :], row_win[t][:, :S], sg[:, t, :], MULT)
         for t in range(PACK):
-            nc.scalar.activation(w_n2[:, t, :], row_win[t][:].indirect(n2_t[:]), COPY)
+            nc.scalar.activation(w_n2[:, t, :], row_win[t][:].indirect(n2_t[:]), COPY, scale=-0.5)
 
         def woven_out(ap):
             return ap.rearrange("p (c i t) -> p c t i", i=4, t=PACK)
@@ -199,11 +198,9 @@ def tile_picked_pqcjmxbekd_none_po_kernel(
             nc.scalar.activation(row_win[t][:, :S], b_ps[t // 2][:, t % 2, :], COPY, scale=0.0625)
         b_n4 = sb("b_n4", [P, PACK, S], F32)
         diff = sb("diff", [P, PACK, S], F32)
-        for v in range(2):
-            pair = slice(2 * v, 2 * v + 2)
-            for t in range(2 * v, 2 * v + 2):
-                nc.scalar.activation(b_n4[:, t, :], row_win[t][:].indirect(n4_t[:]), COPY)
-            nc.vector.scalar_tensor_tensor(diff[:, pair, :], b_ps[v][:], -0.0625, b_n4[:, pair, :], MULT, ADD)
+        for t in range(PACK):
+            nc.scalar.activation(b_n4[:, t, :], row_win[t][:].indirect(n4_t[:]), COPY)
+            nc.gpsimd.tensor_tensor(diff[:, t, :], b_n4[:, t, :], row_win[t][:, :S], SUBTRACT)
 
         y_words = sb("y_words", [P, S], U32)
         y_plane = sb("y_plane", [P, S], U8)

@@ -60,16 +60,15 @@ def tile_picked_pqcjmxbekd_none_po_kernel(
 
         d_byte_win = sb("d_byte_win", [P, G], U8)
         x_byte_win = sb("x_byte_win", [P, T], U8)
+        nc.gpsimd.memset(d_byte_win[:].bitcast(I32), 0)
         nc.vector.memset(x_byte_win[:].bitcast(I32), 0)
 
         row_win = [sb("row_win%d" % t, [P, 2 * S], F32) for t in range(PACK)]
+        b_win = [sb("b_win%d" % t, [P, 2 * S], F32) for t in range(PACK - 1)] + row_win[PACK - 1 :]
         d_word_win = sb("d_word_win", [P, G], U32)
         x_word_win = sb("x_word_win", [P, T], U32)
         k1_t = load_list("k1_t", k1)
-        nc.sync.dma_start(
-            out=d_byte_win[:].bitcast(I32),
-            in_=d_scales[0].bitcast(I32).unsqueeze(1).to_broadcast([16, 8, G // 4]),
-        )
+        nc.sync.dma_start(out=d_byte_win[:].bitcast(I32)[0:P:8, :], in_=d_scales[0].bitcast(I32))
         k2_t = load_list("k2_t", k2)
         sl_t = load_rows(nc.sync, "sl_t", sl)
         th_t = load_rows(nc.sync, "th_t", th)
@@ -108,8 +107,8 @@ def tile_picked_pqcjmxbekd_none_po_kernel(
         nc.gpsimd.tensor_scalar(h_gain[:], gs_t[:], 0.0625, 0.0, MULT, ADD)
         bias2 = minus_product("bias2", sl2_t, th2_t)
 
-        for t in range(PACK):
-            nc.vector.memset(row_win[t][:, S:], 0.0)
+        for win in row_win + b_win[: PACK - 1]:
+            nc.vector.memset(win[:, S:], 0.0)
 
         d_bytes = at(4096, "d_bytes", [P, 2, H], U8)
         nc.vector.tensor_copy(d_bytes[:, 0, :], d_byte_win[:].indirect(k1_t[:]))
@@ -126,11 +125,9 @@ def tile_picked_pqcjmxbekd_none_po_kernel(
         tab_win.append(at(4096, "tab_win3", [P, J], F32))
         nc.sync.dma_start(out=tab_win[3][:], in_=tab_rows[:, 3, :])
 
-        def coded_matrix(name, list_t, picked):
+        def coded_matrix(list_t, picked, words):
             nc.vector.tensor_copy(picked[:], d_word_win[:].indirect(list_t[:]))
-            words = sb(name + "_words", [P, H], U32)
             nc.vector.tensor_copy(dealt(words[:]), listed(picked[:]))
-            return words
 
         def tokens(list_t, words, plane):
             nc.vector.tensor_copy(plane[:], x_byte_win[:].indirect(list_t[:]))
@@ -146,12 +143,14 @@ def tile_picked_pqcjmxbekd_none_po_kernel(
         xq_words = sb("xq_words", [P, S], U32)
         xq_plane = sb("xq_plane", [P, S], U8)
         tokens(offs_t, xq_words, xq_plane)
-        k1_words = coded_matrix("k1", k1_t, at(0, "k1_picked", [P, H], U32))
+        k1_words = sb("k1_words", [P, H], U32)
+        coded_matrix(k1_t, at(0, "k1_picked", [P, H], U32), k1_words)
         h_ps = [psum.tile([P, S], F32, name="h_ps%d" % t) for t in range(PACK)]
         for t in range(PACK):
             product(h_ps[t][:], k1_words, d_plane[:, 0, :], t, xq_words[:], xq_plane[:])
 
-        k2_words = coded_matrix("k2", k2_t, at(4 * S + S + C, "k2_picked", [P, H], U32))
+        k2_words = at(6144, "k2_words", [P, H], U32)
+        coded_matrix(k2_t, at(4 * S + S + C, "k2_picked", [P, H], U32), k2_words)
         x2_words = at(0, "x2_words", [P, S], U32)
         x2_plane = at(4 * S, "x2_plane", [P, S], U8)
         tokens(two_t, x2_words, x2_plane)
@@ -159,9 +158,12 @@ def tile_picked_pqcjmxbekd_none_po_kernel(
         for t in range(PACK):
             product(b_ps[t // 2][:, t % 2, :], k2_words, d_plane[:, 1, :], t, x2_words[:], x2_plane[:])
 
+        for t in range(PACK - 1):
+            nc.vector.tensor_scalar(b_win[t][:, :S], b_ps[t // 2][:, t % 2, :], 0.0625, None, MULT)
+
         cand_plane = at(4 * S + S, "cand_plane", [P, C], U8)
         nc.vector.tensor_copy(dealt(cand_plane[:]), x_byte_win[:].indirect(cand_t[:]))
-        cand_words = at(4 * S + S + C, "cand_words", [P, C], U32)
+        cand_words = at(6144, "cand_words", [P, C], U32)
         nc.vector.tensor_copy(dealt(cand_words[:]), x_word_win[:].indirect(cand_t[:]))
 
         sg = sb("sg", [P, PACK, S], F32)
@@ -185,22 +187,29 @@ def tile_picked_pqcjmxbekd_none_po_kernel(
         def woven_in(ap):
             return ap.rearrange("p t (c i) -> p c t i", i=4)
 
-        z_bf = sb("z_bf", [P, PACK * S], BF16)
-        nc.vector.tensor_tensor(woven_out(z_bf[:]), woven_in(gated[:]), woven_in(w_n2[:]), ADD)
-        z_words = sb("z_words", [P, S], U32)
-        z_plane = sb("z_plane", [P, S], U8)
-        nc.vector.quantize_mx(out=z_words[:].bitcast(FP8X4), scales=z_plane[:], in_=z_bf[:])
-        a_ps = [psum.tile([P, 2, S], F32, name="a_ps%d" % v) for v in range(2)]
-        for t in range(PACK):
-            product(a_ps[t // 2][:, t % 2, :], cand_words, cand_plane, t, z_words[:], z_plane[:])
+        a_ps = []
+        for u in range(HALVES):
+            cols = slice(u * W, (u + 1) * W)
+            z_bf = sb("z_bf%d" % u, [P, PACK * W], BF16)
+            nc.vector.tensor_tensor(woven_out(z_bf[:]), woven_in(gated[:, :, cols]), woven_in(w_n2[:, :, cols]), ADD)
+            z_words = sb("z_words%d" % u, [P, W], U32)
+            z_plane = sb("z_plane%d" % u, [P, W], U8)
+            nc.vector.quantize_mx(out=z_words[:].bitcast(FP8X4), scales=z_plane[:], in_=z_bf[:])
+            acc = psum.tile([P, PACK, W], F32, name="a_ps%d" % u)
+            for t in range(PACK):
+                product(acc[:, t, :], cand_words, cand_plane, t, z_words[:], z_plane[:])
+            a_ps.append(acc)
 
+        nc.scalar.activation(b_win[3][:, :S], b_ps[1][:, 1, :], COPY, scale=0.0625)
+        sg2 = sb("sg2", [P, PACK, S], F32)
         for t in range(PACK):
-            nc.scalar.activation(row_win[t][:, :S], b_ps[t // 2][:, t % 2, :], COPY, scale=0.0625)
-        b_n4 = sb("b_n4", [P, PACK, S], F32)
-        diff = sb("diff", [P, PACK, S], F32)
-        for t in range(PACK):
-            nc.scalar.activation(b_n4[:, t, :], row_win[t][:].indirect(n4_t[:]), COPY)
-            nc.gpsimd.tensor_tensor(diff[:, t, :], b_n4[:, t, :], row_win[t][:, :S], SUBTRACT)
+            nc.scalar.activation(
+                sg2[:, t, :], b_win[t][:].indirect(n3_t[:]), SIGMOID,
+                bias=bias2[:, t : t + 1], scale=sl2_t[:, t : t + 1],
+            )
+        score = [sb("score%d" % u, [P, PACK, W], F32) for u in range(HALVES)]
+        for u in range(HALVES):
+            nc.vector.scalar_tensor_tensor(score[u][:], a_ps[u][:], 0.0625, sg2[:, :, u * W : (u + 1) * W], MULT, MULT)
 
         y_words = sb("y_words", [P, S], U32)
         y_plane = sb("y_plane", [P, S], U8)
@@ -208,24 +217,30 @@ def tile_picked_pqcjmxbekd_none_po_kernel(
         out_words = out_1[0].rearrange("p n t -> p (n t)").bitcast(I32)
         for u in range(HALVES):
             cols = slice(u * W, (u + 1) * W)
-            n3_half = n3_t[:, u * (W // LIST_ROWS) : (u + 1) * (W // LIST_ROWS)]
-            sg2 = sb("sg2_%d" % u, [P, PACK, W], F32)
-            score = sb("score%d" % u, [P, PACK, W], F32)
+            n4_half = n4_t[:, u * (W // LIST_ROWS) : (u + 1) * (W // LIST_ROWS)]
+            b_n4 = sb("b_n4_%d" % u, [P, PACK, W], F32)
+            diff = sb("diff%d" % u, [P, PACK, W], F32)
             y = sb("y%d" % u, [P, PACK, W], F32)
-            for v in range(2):
-                pair = slice(2 * v, 2 * v + 2)
-                for t in range(2 * v, 2 * v + 2):
-                    nc.scalar.activation(
-                        sg2[:, t, :], row_win[t][:].indirect(n3_half), SIGMOID,
-                        bias=bias2[:, t : t + 1], scale=sl2_t[:, t : t + 1],
-                    )
-                nc.vector.scalar_tensor_tensor(score[:, pair, :], a_ps[v][:, :, cols], 0.0625, sg2[:, pair, :], MULT, MULT)
-                nc.vector.tensor_tensor(y[:, pair, :], score[:, pair, :], diff[:, pair, cols], MAX)
-            nc.sync.dma_start(out=out_rows[:, :, cols], in_=y[:])
             y_bf = sb("y_bf%d" % u, [P, PACK * W], BF16)
-            nc.vector.tensor_copy(woven_out(y_bf[:]), woven_in(y[:]))
+            last = u == HALVES - 1
+            for t in range(PACK):
+                nc.scalar.activation(b_n4[:, t, :], b_win[t][:].indirect(n4_half), COPY)
+                if not last:
+                    nc.gpsimd.tensor_tensor(diff[:, t, :], b_n4[:, t, :], b_win[t][:, cols], SUBTRACT)
+                elif t % 2:
+                    pair = slice(t - 1, t + 1)
+                    nc.vector.scalar_tensor_tensor(diff[:, pair, :], b_ps[t // 2][:, :, cols], -0.0625, b_n4[:, pair, :], MULT, ADD)
+                    nc.vector.tensor_tensor(y[:, pair, :], score[u][:, pair, :], diff[:, pair, :], MAX)
+            if not last:
+                nc.vector.tensor_tensor(y[:], score[u][:], diff[:], MAX)
+            nc.sync.dma_start(out=out_rows[:, :, cols], in_=y[:])
+            if last:
+                nc.vector.tensor_copy(woven_out(y_bf[:]), woven_in(y[:]))
+            else:
+                nc.scalar.copy(woven_out(y_bf[:]), woven_in(y[:]))
             nc.vector.quantize_mx(out=y_words[:, cols].bitcast(FP8X4), scales=y_plane[:, cols], in_=y_bf[:])
-            nc.sync.dma_start(out=out_words[:, cols], in_=y_words[:, cols].bitcast(I32))
+            queue = nc.scalar if last else nc.sync
+            queue.dma_start(out=out_words[:, cols], in_=y_words[:, cols].bitcast(I32))
 
         out_scale_rows = out_2[0].bitcast(I32)
         y_plane_i = y_plane[:].bitcast(I32)

from contextlib import ExitStack

import concourse.mybir as mybir

K, T, S, G, H, J, C = 512, 1024, 256, 2048, 512, 512, 512
FLOPS = 2 * K * S * (H + C + H)

F32 = mybir.dt.float32
BF16 = mybir.dt.bfloat16
I32 = mybir.dt.int32
U32 = mybir.dt.uint32
U16 = mybir.dt.uint16
U8 = mybir.dt.uint8
FP8X4 = mybir.dt.float8_e4m3fn_x4
MULT = mybir.AluOpType.mult
ADD = mybir.AluOpType.add
SUBTRACT = mybir.AluOpType.subtract
MAX = mybir.AluOpType.max
COPY = mybir.ActivationFunctionType.Copy
SIGMOID = mybir.ActivationFunctionType.Sigmoid

P = 128
PACK = 4
HALVES = 2
W = S // HALVES
LIST_ROWS = 16


def tile_picked_pqcjmxbekd_none_po_kernel(
    tc, x_words, x_scales, d_words, d_scales, tab, sl, th, gs, sl2, th2,
    offs, k1, n1, n2, cand, two, k2, n3, n4, out_0, out_1, out_2,
):
    nc = tc.nc
    with ExitStack() as ctx:
        keep = ctx.enter_context(tc.tile_pool(name="keep", bufs=1))
        reuse = ctx.enter_context(tc.tile_pool(name="reuse", bufs=1))
        psum = ctx.enter_context(tc.psum_pool(name="psum", bufs=1))

        def sb(name, shape, dtype, tag=None):
            return keep.tile(shape, dtype, name=name, tag=tag or name, align_bytes=64)

        def at(offset, name, shape, dtype):
            return reuse.tile(shape, dtype, name=name, offset=offset, align_bytes=64)

        def load_list(name, src):
            t = keep.tile(list(src.shape), U16, name=name)
            nc.sync.dma_start(t[:], src)
            return t

        def load_rows(eng, name, src):
            t = sb(name, [P, PACK], F32)
            eng.dma_start(out=t[:], in_=src.rearrange("(p t) o -> p (t o)", t=PACK))
            return t

        def dealt(ap):
            return ap.rearrange("p (t m) -> p m t", t=PACK)

        def listed(ap):
            return ap.rearrange("p (m t) -> p m t", t=PACK)

        d_byte_win = sb("d_byte_win", [P, G], U8)
        x_byte_win = sb("x_byte_win", [P, T], U8)
        nc.gpsimd.memset(d_byte_win[:].bitcast(I32), 0)
        nc.vector.memset(x_byte_win[:].bitcast(I32), 0)

        row_win = [sb("row_win%d" % t, [P, 2 * S], F32) for t in range(PACK)]
        b_win = [sb("b_win%d" % t, [P, 2 * S], F32) for t in range(PACK - 1)] + row_win[PACK - 1 :]
        d_word_win = sb("d_word_win", [P, G], U32)
        x_word_win = sb("x_word_win", [P, T], U32)
        k1_t = load_list("k1_t", k1)
        nc.sync.dma_start(out=d_byte_win[:].bitcast(I32)[0:P:8, :], in_=d_scales[0].bitcast(I32))
        k2_t = load_list("k2_t", k2)
        sl_t = load_rows(nc.sync, "sl_t", sl)
        th_t = load_rows(nc.sync, "th_t", th)
        n1_t = load_list("n1_t", n1)
        tab_rows = tab.rearrange("(p t) j -> p t j", t=PACK)
        tab_win = [sb("tab_win%d" % t, [P, J], F32) for t in range(PACK - 1)]
        nc.sync.dma_start(out=tab_win[0][:], in_=tab_rows[:, 0, :])
        nc.sync.dma_start(out=x_word_win[:].bitcast(I32), in_=x_words[0].rearrange("p n t -> p (n t)").bitcast(I32))
        offs_t = load_list("offs_t", offs)
        x_rows = x_scales[0].bitcast(I32)
        for q in range(4):
            nc.sync.dma_start(out=x_byte_win[:].bitcast(I32)[32 * q : 32 * q + 4, :], in_=x_rows[4 * q : 4 * q + 4, :])
        nc.sync.dma_start(out=d_word_win[:].bitcast(I32), in_=d_words[0].rearrange("p n t -> p (n t)").bitcast(I32))
        n2_t = load_list("n2_t", n2)
        n3_t = load_list("n3_t", n3)
        n4_t = load_list("n4_t", n4)
        two_t = load_list("two_t", two)
        cand_t = load_list("cand_t", cand)
        for t in range(1, PACK - 1):
            nc.sync.dma_start(out=tab_win[t][:], in_=tab_rows[:, t, :])

        gs_t = load_rows(nc.gpsimd, "gs_t", gs)
        sl2_t = load_rows(nc.gpsimd, "sl2_t", sl2)
        th2_t = load_rows(nc.gpsimd, "th2_t", th2)

        def minus_product(name, u, v):
            prod = sb(name + "_pos", [P, PACK], F32)
            nc.gpsimd.tensor_tensor(prod[:], u[:], v[:], MULT)
            neg = sb(name, [P, PACK], F32)
            nc.gpsimd.tensor_scalar(neg[:], prod[:], -1.0, 0.0, MULT, ADD)
            return neg

        bias1 = sb("bias1", [P, PACK], F32)
        nc.vector.scalar_tensor_tensor(bias1[:], sl_t[:], -1.0, th_t[:], MULT, MULT)
        h_gain = sb("h_gain", [P, PACK], F32)
        nc.gpsimd.tensor_scalar(h_gain[:], gs_t[:], 0.0625, 0.0, MULT, ADD)
        bias2 = minus_product("bias2", sl2_t, th2_t)

        for win in row_win + b_win[: PACK - 1]:
            nc.vector.memset(win[:, S:], 0.0)

        d_bytes = at(4096, "d_bytes", [P, 2, H], U8)
        nc.vector.tensor_copy(d_bytes[:, 0, :], d_byte_win[:].indirect(k1_t[:]))
        nc.vector.tensor_copy(d_bytes[:, 1, :], d_byte_win[:].indirect(k2_t[:]))
        d_plane = sb("d_plane", [P, 2, H], U8)
        nc.vector.tensor_copy(
            d_plane[:].rearrange("p l (t m) -> p l m t", t=PACK),
            d_bytes[:].rearrange("p l (m t) -> p l m t", t=PACK),
        )
        d_plane_i = d_plane[:].rearrange("p l h -> p (l h)").bitcast(I32)
        for r in range(1, 4):
            nc.sync.dma_start(out=d_plane_i[r:P:32, :], in_=d_plane_i[8 * r : P : 32, :])

        tab_win.append(at(4096, "tab_win3", [P, J], F32))
        nc.sync.dma_start(out=tab_win[3][:], in_=tab_rows[:, 3, :])

        def coded_matrix(list_t, picked, words):
            nc.vector.tensor_copy(picked[:], d_word_win[:].indirect(list_t[:]))
            nc.vector.tensor_copy(dealt(words[:]), listed(picked[:]))

        def tokens(list_t, words, plane):
            nc.vector.tensor_copy(plane[:], x_byte_win[:].indirect(list_t[:]))
            nc.vector.tensor_copy(words[:], x_word_win[:].indirect(list_t[:]))

        def product(out, words, plane, t, rhs_words, rhs_plane):
            cols = slice(t * P, (t + 1) * P)
            nc.tensor.matmul_mx(
                out=out, lhsT=words[:, cols].bitcast(FP8X4), lhsT_scale=plane[:, cols],
                rhs=rhs_words.bitcast(FP8X4), rhs_scale=rhs_plane, start=True, stop=True,
            )

        xq_words = sb("xq_words", [P, S], U32)
        xq_plane = sb("xq_plane", [P, S], U8)
        tokens(offs_t, xq_words, xq_plane)
        k1_words = sb("k1_words", [P, H], U32)
        coded_matrix(k1_t, at(0, "k1_picked", [P, H], U32), k1_words)
        h_ps = [psum.tile([P, S], F32, name="h_ps%d" % t) for t in range(PACK)]
        for t in range(PACK):
            product(h_ps[t][:], k1_words, d_plane[:, 0, :], t, xq_words[:], xq_plane[:])

        k2_words = at(6144, "k2_words", [P, H], U32)
        coded_matrix(k2_t, at(4 * S + S + C, "k2_picked", [P, H], U32), k2_words)
        x2_words = at(0, "x2_words", [P, S], U32)
        x2_plane = at(4 * S, "x2_plane", [P, S], U8)
        tokens(two_t, x2_words, x2_plane)
        b_ps = [psum.tile([P, 2, S], F32, name="b_ps%d" % u) for u in range(2)]
        for t in range(PACK):
            product(b_ps[t // 2][:, t % 2, :], k2_words, d_plane[:, 1, :], t, x2_words[:], x2_plane[:])

        for t in range(PACK - 1):
            nc.vector.tensor_scalar(b_win[t][:, :S], b_ps[t // 2][:, t % 2, :], 0.0625, None, MULT)

        cand_plane = at(4 * S + S, "cand_plane", [P, C], U8)
        nc.vector.tensor_copy(dealt(cand_plane[:]), x_byte_win[:].indirect(cand_t[:]))
        cand_words = at(6144, "cand_words", [P, C], U32)
        nc.vector.tensor_copy(dealt(cand_words[:]), x_word_win[:].indirect(cand_t[:]))

        sg = sb("sg", [P, PACK, S], F32)
        for t in range(PACK):
            nc.scalar.activation(
                sg[:, t, :], tab_win[t][:].indirect(n1_t[:]), SIGMOID,
                bias=bias1[:, t : t + 1], scale=sl_t[:, t : t + 1],
            )

        gated = sb("gated", [P, PACK, S], F32)
        w_n2 = sb("w_n2", [P, PACK, S], F32)
        for t in range(PACK):
            nc.scalar.activation(row_win[t][:, :S], h_ps[t][:], COPY, scale=h_gain[:, t : t + 1])
            nc.gpsimd.tensor_tensor(gated[:, t, :], row_win[t][:, :S], sg[:, t, :], MULT)
        for t in range(PACK):
            nc.scalar.activation(w_n2[:, t, :], row_win[t][:].indirect(n2_t[:]), COPY, scale=-0.5)

        def woven_out(ap):
            return ap.rearrange("p (c i t) -> p c t i", i=4, t=PACK)

        def woven_in(ap):
            return ap.rearrange("p t (c i) -> p c t i", i=4)

        a_ps = []
        for u in range(HALVES):
            cols = slice(u * W, (u + 1) * W)
            z_bf = sb("z_bf%d" % u, [P, PACK * W], BF16)
            nc.vector.tensor_tensor(woven_out(z_bf[:]), woven_in(gated[:, :, cols]), woven_in(w_n2[:, :, cols]), ADD)
            z_words = sb("z_words%d" % u, [P, W], U32)
            z_plane = sb("z_plane%d" % u, [P, W], U8)
            nc.vector.quantize_mx(out=z_words[:].bitcast(FP8X4), scales=z_plane[:], in_=z_bf[:])
            acc = psum.tile([P, PACK, W], F32, name="a_ps%d" % u)
            for t in range(PACK):
                product(acc[:, t, :], cand_words, cand_plane, t, z_words[:], z_plane[:])
            a_ps.append(acc)

        nc.scalar.activation(b_win[3][:, :S], b_ps[1][:, 1, :], COPY, scale=0.0625)
        sg2 = sb("sg2", [P, PACK, S], F32)
        for t in range(PACK):
            nc.scalar.activation(
                sg2[:, t, :], b_win[t][:].indirect(n3_t[:]), SIGMOID,
                bias=bias2[:, t : t + 1], scale=sl2_t[:, t : t + 1],
            )
        score = [sb("score%d" % u, [P, PACK, W], F32) for u in range(HALVES)]
        for u in range(HALVES):
            nc.vector.scalar_tensor_tensor(score[u][:], a_ps[u][:], 0.0625, sg2[:, :, u * W : (u + 1) * W], MULT, MULT)

        y_words = sb("y_words", [P, S], U32)
        y_plane = sb("y_plane", [P, S], U8)
        out_rows = out_0.rearrange("(p t) j -> p t j", t=PACK)
        out_words = out_1[0].rearrange("p n t -> p (n t)").bitcast(I32)
        for u in range(HALVES):
            cols = slice(u * W, (u + 1) * W)
            n4_half = n4_t[:, u * (W // LIST_ROWS) : (u + 1) * (W // LIST_ROWS)]
            b_n4 = sb("b_n4_%d" % u, [P, PACK, W], F32)
            diff = sb("diff%d" % u, [P, PACK, W], F32)
            y = sb("y%d" % u, [P, PACK, W], F32)
            y_bf = sb("y_bf%d" % u, [P, PACK * W], BF16)
            last = u == HALVES - 1
            for t in range(PACK):
                nc.scalar.activation(b_n4[:, t, :], b_win[t][:].indirect(n4_half), COPY)
                if not last:
                    nc.gpsimd.tensor_tensor(diff[:, t, :], b_n4[:, t, :], b_win[t][:, cols], SUBTRACT)
                elif t % 2:
                    pair = slice(t - 1, t + 1)
                    nc.vector.scalar_tensor_tensor(diff[:, pair, :], b_ps[t // 2][:, :, cols], -0.0625, b_n4[:, pair, :], MULT, ADD)
                    nc.vector.tensor_tensor(y[:, pair, :], score[u][:, pair, :], diff[:, pair, :], MAX)
            if not last:
                nc.vector.tensor_tensor(y[:], score[u][:], diff[:], MAX)
            nc.sync.dma_start(out=out_rows[:, :, cols], in_=y[:])
            if last:
                nc.vector.tensor_copy(woven_out(y_bf[:]), woven_in(y[:]))
            else:
                nc.scalar.copy(woven_out(y_bf[:]), woven_in(y[:]))
            nc.vector.quantize_mx(out=y_words[:, cols].bitcast(FP8X4), scales=y_plane[:, cols], in_=y_bf[:])
            queue = nc.scalar if last else nc.sync
            queue.dma_start(out=out_words[:, cols], in_=y_words[:, cols].bitcast(I32))

        out_scale_rows = out_2[0].bitcast(I32)
        y_plane_i = y_plane[:].bitcast(I32)
        for q in range(4):
            eng = nc.scalar if q % 2 else nc.sync
            eng.dma_start(out=out_scale_rows[4 * q : 4 * q + 4, :], in_=y_plane_i[32 * q : 32 * q + 4, :])
